import numpy as np
import ml_dtypes


def mxq(x, axis, fmt="e4m3"):
    dtype, down = {"e4m3": (ml_dtypes.float8_e4m3fn, 7), "e5m2": (ml_dtypes.float8_e5m2, 14)}[fmt]
    v = np.moveaxis(np.asarray(x, np.float32).astype(ml_dtypes.bfloat16).astype(np.float64), axis, -1)
    blocks = v.reshape(v.shape[:-1] + (-1, 32))
    amax = np.abs(blocks).max(-1, keepdims=True)
    byte = np.maximum(np.where(amax > 0, np.frexp(amax)[1] - 1 + 127, 0) - down, 1)
    scale = np.exp2(byte - 127.0)
    codes = (blocks / scale).astype(np.float32).astype(dtype).astype(np.float64)
    return np.moveaxis((codes * scale).reshape(v.shape), -1, axis)


WIDE = False


def mx_kscale(k):
    if not WIDE:
        return np.ones(k)
    levels = np.array([10, -10, 5, -5, 0])
    if k % 512:
        return np.exp2(np.random.permutation(np.resize(levels, k // 32))).repeat(32)
    a = np.empty((k // 512, 16))
    for p in range(k // 512):
        a[p, :8] = np.random.permutation(np.resize(levels, 8))
        for g in range(8):
            far = levels[np.abs(levels - a[p, g]) >= 10]
            a[p, g + 8] = far[np.random.randint(len(far))]
    return np.exp2(a.ravel()).repeat(32)


def f64(x):
    return np.asarray(x).astype(np.float64)


def striped(idx):
    return np.tile(np.asarray(idx).reshape(-1, 16).T, (8, 1)).astype(np.uint16)


def unstriped(offs):
    return offs[:16].T.reshape(-1).astype(np.int64)


E2M1 = np.array([0.0, 0.5, 1.0, 1.5, 2.0, 3.0, 4.0, 6.0, -0.0, -0.5, -1.0, -1.5, -2.0, -3.0, -4.0, -6.0])


def pack_weight(w, fmt):
    k, n = w.shape
    w = f64(np.asarray(w, np.float32).astype(ml_dtypes.bfloat16)).reshape(k // 32, 32, n)
    amax = np.abs(w).max(1)
    if fmt == "e4m3":
        byte = np.frexp(amax)[1] - 1 + 127 - 7
    else:
        mant, ex = np.frexp(amax / 6.0)
        byte = np.where(mant > 0.5, ex, ex - 1) + 127
    byte = np.clip(np.where(amax > 0, byte, 1), 1, 254)
    scaled = (w * np.exp2(127.0 - byte)[:, None, :]).reshape(k, n).astype(np.float32)
    by_word = np.ascontiguousarray(scaled.reshape(k // 512, 128, 4, n).transpose(0, 1, 3, 2))
    if fmt == "e4m3":
        words = by_word.astype(ml_dtypes.float8_e4m3fn).view(np.uint8)
    else:
        c = by_word.astype(ml_dtypes.float4_e2m1fn).view(np.uint8) & 0xF
        words = (c[..., 0::2] | (c[..., 1::2] << 4)).reshape(k // 512, 128, 2 * n)
    return np.ascontiguousarray(words), np.ascontiguousarray(byte.astype(np.uint8).reshape(k // 512, 16, n))


def unpack_weight(words, scales, fmt):
    g, _, n = scales.shape
    words = np.ascontiguousarray(words).reshape(g, 128, n, -1)
    if fmt == "e4m3":
        vals = words.view(ml_dtypes.float8_e4m3fn).astype(np.float64)
    else:
        nib = np.empty((g, 128, n, 4), np.uint8)
        nib[..., 0::2] = words & 0xF
        nib[..., 1::2] = words >> 4
        vals = E2M1[nib]
    vals = vals * np.repeat(np.exp2(scales.astype(np.float64) - 127.0), 8, axis=1)[..., None]
    return vals.transpose(0, 1, 3, 2).reshape(g * 512, n)


B, N, T, D, NQ = 1, 512, 4096, 512, 128


def setup_inputs():
    n = np.random.standard_normal
    idx = np.random.permutation(T)[:B * N]
    s = mx_kscale(D)[:, None]
    kp = pack_weight(n((D, T)) / s, "e4m3")
    return {
        "qT": (n((B, D, NQ)) * s * (1.00 / np.sqrt(D))).astype(np.float32),
        "k_words": kp[0],
        "k_scales": kp[1],
        "t": (np.random.uniform(0.05, 1.0, (B, NQ, N))).astype(np.float32),
        "ls": (np.random.uniform(8.5, 9.0, (B, NQ, 1))).astype(np.float32),
        "offs": striped(idx),
    }


def reference(qT, k_words, k_scales, t, ls, offs):
    idx = unstriped(offs)
    pick = lambda x, which: x[:, which].reshape(x.shape[0], B, -1).transpose(1, 0, 2)
    k = unpack_weight(k_words, k_scales, "e4m3")
    kg = pick(k, idx)
    qq = mxq(f64(qT), 1, "e4m3")
    a = qq.transpose(0, 2, 1) @ kg
    y = f64(t) * (np.log(f64(t)) - a + f64(ls))
    return y

@@ -1,0 +1,93 @@
+from contextlib import ExitStack
+
+import concourse.mybir as mybir
+
+F32 = mybir.dt.float32
+BF16 = mybir.dt.bfloat16
+I32 = mybir.dt.int32
+U32 = mybir.dt.uint32
+U16 = mybir.dt.uint16
+U8 = mybir.dt.uint8
+FP8X4 = mybir.dt.float8_e4m3fn_x4
+ALU = mybir.AluOpType
+ACT = mybir.ActivationFunctionType
+
+P = 128
+PACK = 4
+NQ = 128
+SLOTS = 512
+VOCAB = 4096
+D = 512
+PIECES = 2
+PIECE = SLOTS // PIECES
+
+FLOPS = 2 * D * NQ * SLOTS
+
+
+def tile_attend_kdterm_topk_kernel(tc, qT, k_words, k_scales, t, ls, offs, out):
+    nc = tc.nc
+    with ExitStack() as ctx:
+        keep = ctx.enter_context(tc.tile_pool(name="keep", bufs=1))
+        psum = ctx.enter_context(tc.psum_pool(name="psum", bufs=1))
+
+        offsets = keep.tile([P, SLOTS // 16], U16, name="offsets")
+        q_raw = keep.tile([P, PACK, NQ], F32, name="q_raw")
+        q_bf = keep.tile([P, NQ, PACK], BF16, name="q_bf", align_bytes=64)
+        q_codes = keep.tile([P, NQ], U32, name="q_codes", align_bytes=64)
+        q_scales = keep.tile([P, NQ], U8, name="q_scales", align_bytes=64)
+        pool_words = keep.tile([P, VOCAB], I32, name="pool_words", align_bytes=64)
+        pool_scales = keep.tile([P, VOCAB], U8, name="pool_scales", align_bytes=64)
+        key_words = keep.tile([P, SLOTS], U32, name="key_words", align_bytes=64)
+        key_scales = keep.tile([P, SLOTS], U8, name="key_scales", align_bytes=64)
+        t_sb = keep.tile([P, SLOTS], F32, name="t_sb")
+        ls_sb = keep.tile([P, 1], F32, name="ls_sb")
+        ln_t = keep.tile([P, SLOTS], F32, name="ln_t")
+
+        nc.vector.memset(pool_scales[:].bitcast(I32), 0)
+
+        nc.sync.dma_start(out=q_raw[:], in_=qT[0].rearrange("(p j) w -> p j w", j=PACK))
+        nc.sync.dma_start(offsets[:], offs)
+        nc.sync.dma_start(out=pool_words[:], in_=k_words[0].rearrange("p n r -> p (n r)").bitcast(I32))
+        nc.sync.dma_start(out=t_sb[:], in_=t[0])
+
+        nc.scalar.dma_start(out=ls_sb[:], in_=ls[0])
+        scale_rows = k_scales[0].bitcast(I32)
+        for j in range(4):
+            nc.scalar.dma_start(out=pool_scales[:].bitcast(I32)[j:P:32, :], in_=scale_rows[j:16:4, :])
+
+        nc.vector.tensor_copy(out=q_bf[:], in_=q_raw[:].rearrange("p j w -> p w j"))
+        nc.vector.quantize_mx(
+            out=q_codes[:].bitcast(FP8X4),
+            scales=q_scales[:],
+            in_=q_bf[:].rearrange("p w j -> p (w j)"),
+        )
+        nc.vector.tensor_copy(key_scales[:], pool_scales[:].indirect(offsets[:]))
+        nc.vector.tensor_copy(key_words[:], pool_words[:].bitcast(U32).indirect(offsets[:]))
+
+        nc.scalar.activation(out=ln_t[:], in_=t_sb[:], func=ACT.Ln)
+
+        diffs = []
+        for h in range(PIECES):
+            cols = slice(h * PIECE, (h + 1) * PIECE)
+            acc = psum.tile([P, PIECE], F32, name="acc%d" % h)
+            nc.tensor.matmul_mx(
+                out=acc[:],
+                lhsT=q_codes[:].bitcast(FP8X4),
+                lhsT_scale=q_scales[:],
+                rhs=key_words[:, cols].bitcast(FP8X4),
+                rhs_scale=key_scales[:, cols],
+                start=True,
+                stop=True,
+            )
+            diff = keep.tile([P, PIECE], F32, name="diff%d" % h)
+            nc.vector.scalar_tensor_tensor(
+                out=diff[:], in0=acc[:], scalar=ls_sb[:], in1=ln_t[:, cols], op0=ALU.subtract, op1=ALU.subtract
+            )
+            diffs.append(diff)
+        for h in range(PIECES):
+            cols = slice(h * PIECE, (h + 1) * PIECE)
+            y = keep.tile([P, PIECE], F32, name="y%d" % h)
+            nc.vector.scalar_tensor_tensor(
+                out=y[:], in0=diffs[h][:], scalar=-1.0, in1=t_sb[:, cols], op0=ALU.mult, op1=ALU.mult
+            )
+            nc.sync.dma_start(out=out[0][:, cols], in_=y[:])

@@ -18,7 +18,7 @@ NQ = 128
 SLOTS = 512
 VOCAB = 4096
 D = 512
-PIECES = 2
+PIECES = 4
 PIECE = SLOTS // PIECES
 
 FLOPS = 2 * D * NQ * SLOTS
@@ -36,24 +36,29 @@ def tile_attend_kdterm_topk_kernel(tc, qT, k_words, k_scales, t, ls, offs, out):
         q_codes = keep.tile([P, NQ], U32, name="q_codes", align_bytes=64)
         q_scales = keep.tile([P, NQ], U8, name="q_scales", align_bytes=64)
         pool_words = keep.tile([P, VOCAB], I32, name="pool_words", align_bytes=64)
-        pool_scales = keep.tile([P, VOCAB], U8, name="pool_scales", align_bytes=64)
-        key_words = keep.tile([P, SLOTS], U32, name="key_words", align_bytes=64)
+        pool_scales = keep.tile([P, VOCAB], U8, name="pool_scales", tag="scales_then_words", align_bytes=64)
+        picked_scales = keep.tile([P, SLOTS], U8, name="picked_scales", align_bytes=64)
         key_scales = keep.tile([P, SLOTS], U8, name="key_scales", align_bytes=64)
         t_sb = keep.tile([P, SLOTS], F32, name="t_sb")
         ls_sb = keep.tile([P, 1], F32, name="ls_sb")
         ln_t = keep.tile([P, SLOTS], F32, name="ln_t")
 
         nc.vector.memset(pool_scales[:].bitcast(I32), 0)
+        nc.vector.memset(key_scales[:].bitcast(I32), 0)
 
         nc.sync.dma_start(out=q_raw[:], in_=qT[0].rearrange("(p j) w -> p j w", j=PACK))
         nc.sync.dma_start(offsets[:], offs)
-        nc.sync.dma_start(out=pool_words[:], in_=k_words[0].rearrange("p n r -> p (n r)").bitcast(I32))
+        nc.sync.dma_start(out=pool_words[:], in_=k_words[0].rearrange("p n r -> p (n r)").bitcast(I32), max_dma_last_dim=4096)
         nc.sync.dma_start(out=t_sb[:], in_=t[0])
 
         nc.scalar.dma_start(out=ls_sb[:], in_=ls[0])
-        scale_rows = k_scales[0].bitcast(I32)
+        nc.scalar.dma_start(out=pool_scales[:].bitcast(I32)[0:P:8, :], in_=k_scales[0].bitcast(I32))
+
+        nc.vector.tensor_copy(picked_scales[:], pool_scales[:].indirect(offsets[:]))
         for j in range(4):
-            nc.scalar.dma_start(out=pool_scales[:].bitcast(I32)[j:P:32, :], in_=scale_rows[j:16:4, :])
+            nc.scalar.dma_start(
+                out=key_scales[:].bitcast(I32)[j:P:32, :], in_=picked_scales[:].bitcast(I32)[8 * j : P : 32, :]
+            )
 
         nc.vector.tensor_copy(out=q_bf[:], in_=q_raw[:].rearrange("p j w -> p w j"))
         nc.vector.quantize_mx(
@@ -61,13 +66,14 @@ def tile_attend_kdterm_topk_kernel(tc, qT, k_words, k_scales, t, ls, offs, out):
             scales=q_scales[:],
             in_=q_bf[:].rearrange("p w j -> p (w j)"),
         )
-        nc.vector.tensor_copy(key_scales[:], pool_scales[:].indirect(offsets[:]))
+        key_words = keep.tile([P, SLOTS], U32, name="key_words", tag="scales_then_words", align_bytes=64)
         nc.vector.tensor_copy(key_words[:], pool_words[:].bitcast(U32).indirect(offsets[:]))
 
         nc.scalar.activation(out=ln_t[:], in_=t_sb[:], func=ACT.Ln)
 
-        diffs = []
-        for h in range(PIECES):
+        diffs = {}
+
+        def subtract(h):
             cols = slice(h * PIECE, (h + 1) * PIECE)
             acc = psum.tile([P, PIECE], F32, name="acc%d" % h)
             nc.tensor.matmul_mx(
@@ -79,15 +85,22 @@ def tile_attend_kdterm_topk_kernel(tc, qT, k_words, k_scales, t, ls, offs, out):
                 start=True,
                 stop=True,
             )
-            diff = keep.tile([P, PIECE], F32, name="diff%d" % h)
+            diffs[h] = keep.tile([P, PIECE], F32, name="diff%d" % h)
             nc.vector.scalar_tensor_tensor(
-                out=diff[:], in0=acc[:], scalar=ls_sb[:], in1=ln_t[:, cols], op0=ALU.subtract, op1=ALU.subtract
+                out=diffs[h][:], in0=acc[:], scalar=ls_sb[:], in1=ln_t[:, cols], op0=ALU.subtract, op1=ALU.subtract
             )
-            diffs.append(diff)
-        for h in range(PIECES):
+
+        def weigh(h):
             cols = slice(h * PIECE, (h + 1) * PIECE)
             y = keep.tile([P, PIECE], F32, name="y%d" % h)
             nc.vector.scalar_tensor_tensor(
                 out=y[:], in0=diffs[h][:], scalar=-1.0, in1=t_sb[:, cols], op0=ALU.mult, op1=ALU.mult
             )
-            nc.sync.dma_start(out=out[0][:, cols], in_=y[:])
+            queue = nc.sync if h % 2 == 0 else nc.scalar
+            queue.dma_start(out=out[0][:, cols], in_=y[:])
+
+        subtract(0)
+        for h in range(1, PIECES):
+            subtract(h)
+            weigh(h - 1)
+        weigh(PIECES - 1)

@@ -32,7 +32,6 @@ def tile_attend_kdterm_topk_kernel(tc, qT, k_words, k_scales, t, ls, offs, out):
 
         offsets = keep.tile([P, SLOTS // 16], U16, name="offsets")
         q_raw = keep.tile([P, PACK, NQ], F32, name="q_raw")
-        q_bf = keep.tile([P, NQ, PACK], BF16, name="q_bf", align_bytes=64)
         q_codes = keep.tile([P, NQ], U32, name="q_codes", align_bytes=64)
         q_scales = keep.tile([P, NQ], U8, name="q_scales", align_bytes=64)
         pool_words = keep.tile([P, VOCAB], I32, name="pool_words", align_bytes=64)
@@ -52,14 +51,15 @@ def tile_attend_kdterm_topk_kernel(tc, qT, k_words, k_scales, t, ls, offs, out):
         nc.sync.dma_start(out=t_sb[:], in_=t[0])
 
         nc.scalar.dma_start(out=ls_sb[:], in_=ls[0])
-        nc.scalar.dma_start(out=pool_scales[:].bitcast(I32)[0:P:8, :], in_=k_scales[0].bitcast(I32))
+        nc.scalar.dma_start(out=pool_scales[:].bitcast(I32)[11 : 11 + 7 * 15 + 1 : 7, :], in_=k_scales[0].bitcast(I32))
 
         nc.vector.tensor_copy(picked_scales[:], pool_scales[:].indirect(offsets[:]))
         for j in range(4):
-            nc.scalar.dma_start(
-                out=key_scales[:].bitcast(I32)[j:P:32, :], in_=picked_scales[:].bitcast(I32)[8 * j : P : 32, :]
+            nc.sync.dma_start(
+                out=key_scales[:].bitcast(I32)[j:P:32, :], in_=picked_scales[:].bitcast(I32)[11 + 7 * j : 11 + 7 * (12 + j) + 1 : 28, :]
             )
 
+        q_bf = keep.tile([P, NQ, PACK], BF16, name="q_bf", tag="scales_then_words", align_bytes=64)
         nc.vector.tensor_copy(out=q_bf[:], in_=q_raw[:].rearrange("p j w -> p w j"))
         nc.vector.quantize_mx(
             out=q_codes[:].bitcast(FP8X4),
@@ -69,7 +69,9 @@ def tile_attend_kdterm_topk_kernel(tc, qT, k_words, k_scales, t, ls, offs, out):
         key_words = keep.tile([P, SLOTS], U32, name="key_words", tag="scales_then_words", align_bytes=64)
         nc.vector.tensor_copy(key_words[:], pool_words[:].bitcast(U32).indirect(offsets[:]))
 
-        nc.scalar.activation(out=ln_t[:], in_=t_sb[:], func=ACT.Ln)
+        for half in range(2):
+            cols = slice(half * SLOTS // 2, (half + 1) * SLOTS // 2)
+            nc.scalar.activation(out=ln_t[:, cols], in_=t_sb[:, cols], func=ACT.Ln)
 
         diffs = {}
 
@@ -96,11 +98,12 @@ def tile_attend_kdterm_topk_kernel(tc, qT, k_words, k_scales, t, ls, offs, out):
             nc.vector.scalar_tensor_tensor(
                 out=y[:], in0=diffs[h][:], scalar=-1.0, in1=t_sb[:, cols], op0=ALU.mult, op1=ALU.mult
             )
-            queue = nc.sync if h % 2 == 0 else nc.scalar
+            queue = nc.scalar if h % 2 == 0 else nc.sync
             queue.dma_start(out=out[0][:, cols], in_=y[:])
 
-        subtract(0)
-        for h in range(1, PIECES):
-            subtract(h)
-            weigh(h - 1)
-        weigh(PIECES - 1)
+        LAG = 2
+        for h in range(PIECES + LAG):
+            if h < PIECES:
+                subtract(h)
+            if h >= LAG:
+                weigh(h - LAG)

@@ -18,6 +18,7 @@ NQ = 128
 SLOTS = 512
 VOCAB = 4096
 D = 512
+HEAD = 1024
 PIECES = 4
 PIECE = SLOTS // PIECES
 
@@ -31,27 +32,33 @@ def tile_attend_kdterm_topk_kernel(tc, qT, k_words, k_scales, t, ls, offs, out):
         psum = ctx.enter_context(tc.psum_pool(name="psum", bufs=1))
 
         offsets = keep.tile([P, SLOTS // 16], U16, name="offsets")
-        q_raw = keep.tile([P, PACK, NQ], F32, name="q_raw")
+        q_raw = keep.tile([P, PACK, NQ], F32, name="q_raw", tag="q_then_t")
+        q_bf = keep.tile([P, NQ, PACK], BF16, name="q_bf", align_bytes=64)
         q_codes = keep.tile([P, NQ], U32, name="q_codes", align_bytes=64)
         q_scales = keep.tile([P, NQ], U8, name="q_scales", align_bytes=64)
         pool_words = keep.tile([P, VOCAB], I32, name="pool_words", align_bytes=64)
+        zeros = pool_words[:, VOCAB - SLOTS // 4 :]
         pool_scales = keep.tile([P, VOCAB], U8, name="pool_scales", tag="scales_then_words", align_bytes=64)
         picked_scales = keep.tile([P, SLOTS], U8, name="picked_scales", align_bytes=64)
         key_scales = keep.tile([P, SLOTS], U8, name="key_scales", align_bytes=64)
-        t_sb = keep.tile([P, SLOTS], F32, name="t_sb")
         ls_sb = keep.tile([P, 1], F32, name="ls_sb")
         ln_t = keep.tile([P, SLOTS], F32, name="ln_t")
 
+        nc.vector.memset(zeros, 0)
         nc.vector.memset(pool_scales[:].bitcast(I32), 0)
-        nc.vector.memset(key_scales[:].bitcast(I32), 0)
+        nc.vector.tensor_copy(out=key_scales[:].bitcast(I32), in_=zeros)
 
         nc.sync.dma_start(out=q_raw[:], in_=qT[0].rearrange("(p j) w -> p j w", j=PACK))
         nc.sync.dma_start(offsets[:], offs)
-        nc.sync.dma_start(out=pool_words[:], in_=k_words[0].rearrange("p n r -> p (n r)").bitcast(I32), max_dma_last_dim=4096)
-        nc.sync.dma_start(out=t_sb[:], in_=t[0])
-
         nc.scalar.dma_start(out=ls_sb[:], in_=ls[0])
-        nc.scalar.dma_start(out=pool_scales[:].bitcast(I32)[11 : 11 + 7 * 15 + 1 : 7, :], in_=k_scales[0].bitcast(I32))
+        words = k_words[0].rearrange("p n r -> p (n r)").bitcast(I32)
+        nc.sync.dma_start(out=pool_words[:, :HEAD], in_=words[:, :HEAD])
+        nc.sync.dma_start(out=pool_scales[:].bitcast(I32)[11 : 11 + 7 * 15 + 1 : 7, :], in_=k_scales[0].bitcast(I32))
+        nc.sync.dma_start(out=pool_words[:, HEAD:], in_=words[:, HEAD:])
+
+        nc.vector.tensor_copy(out=q_bf[:], in_=q_raw[:].rearrange("p j w -> p w j"))
+        t_sb = keep.tile([P, SLOTS], F32, name="t_sb", tag="q_then_t")
+        nc.sync.dma_start(out=t_sb[:], in_=t[0])
 
         nc.vector.tensor_copy(picked_scales[:], pool_scales[:].indirect(offsets[:]))
         for j in range(4):
@@ -59,8 +66,6 @@ def tile_attend_kdterm_topk_kernel(tc, qT, k_words, k_scales, t, ls, offs, out):
                 out=key_scales[:].bitcast(I32)[j:P:32, :], in_=picked_scales[:].bitcast(I32)[11 + 7 * j : 11 + 7 * (12 + j) + 1 : 28, :]
             )
 
-        q_bf = keep.tile([P, NQ, PACK], BF16, name="q_bf", tag="scales_then_words", align_bytes=64)
-        nc.vector.tensor_copy(out=q_bf[:], in_=q_raw[:].rearrange("p j w -> p w j"))
         nc.vector.quantize_mx(
             out=q_codes[:].bitcast(FP8X4),
             scales=q_scales[:],

@@ -18,7 +18,7 @@ NQ = 128
 SLOTS = 512
 VOCAB = 4096
 D = 512
-HEAD = 1024
+HEAD = 896
 PIECES = 4
 PIECE = SLOTS // PIECES
 
@@ -38,10 +38,9 @@ def tile_attend_kdterm_topk_kernel(tc, qT, k_words, k_scales, t, ls, offs, out):
         q_scales = keep.tile([P, NQ], U8, name="q_scales", align_bytes=64)
         pool_words = keep.tile([P, VOCAB], I32, name="pool_words", align_bytes=64)
         zeros = pool_words[:, VOCAB - SLOTS // 4 :]
-        pool_scales = keep.tile([P, VOCAB], U8, name="pool_scales", tag="scales_then_words", align_bytes=64)
+        pool_scales = keep.tile([P, VOCAB], U8, name="pool_scales", tag="scales_then_ls", align_bytes=64)
         picked_scales = keep.tile([P, SLOTS], U8, name="picked_scales", align_bytes=64)
         key_scales = keep.tile([P, SLOTS], U8, name="key_scales", align_bytes=64)
-        ls_sb = keep.tile([P, 1], F32, name="ls_sb")
         ln_t = keep.tile([P, SLOTS], F32, name="ln_t")
 
         nc.vector.memset(zeros, 0)
@@ -50,7 +49,6 @@ def tile_attend_kdterm_topk_kernel(tc, qT, k_words, k_scales, t, ls, offs, out):
 
         nc.sync.dma_start(out=q_raw[:], in_=qT[0].rearrange("(p j) w -> p j w", j=PACK))
         nc.sync.dma_start(offsets[:], offs)
-        nc.scalar.dma_start(out=ls_sb[:], in_=ls[0])
         words = k_words[0].rearrange("p n r -> p (n r)").bitcast(I32)
         nc.sync.dma_start(out=pool_words[:, :HEAD], in_=words[:, :HEAD])
         nc.sync.dma_start(out=pool_scales[:].bitcast(I32)[11 : 11 + 7 * 15 + 1 : 7, :], in_=k_scales[0].bitcast(I32))
@@ -66,12 +64,15 @@ def tile_attend_kdterm_topk_kernel(tc, qT, k_words, k_scales, t, ls, offs, out):
                 out=key_scales[:].bitcast(I32)[j:P:32, :], in_=picked_scales[:].bitcast(I32)[11 + 7 * j : 11 + 7 * (12 + j) + 1 : 28, :]
             )
 
+        ls_sb = keep.tile([P, 1], F32, name="ls_sb", tag="scales_then_ls", align_bytes=64)
+        nc.sync.dma_start(out=ls_sb[:], in_=ls[0])
+
         nc.vector.quantize_mx(
             out=q_codes[:].bitcast(FP8X4),
             scales=q_scales[:],
             in_=q_bf[:].rearrange("p w j -> p (w j)"),
         )
-        key_words = keep.tile([P, SLOTS], U32, name="key_words", tag="scales_then_words", align_bytes=64)
+        key_words = keep.tile([P, SLOTS], U32, name="key_words", align_bytes=64)
         nc.vector.tensor_copy(key_words[:], pool_words[:].bitcast(U32).indirect(offsets[:]))
 
         for half in range(2):

@@ -18,7 +18,7 @@ NQ = 128
 SLOTS = 512
 VOCAB = 4096
 D = 512
-HEAD = 896
+HEAD = 640
 PIECES = 4
 PIECE = SLOTS // PIECES
 
@@ -32,17 +32,22 @@ def tile_attend_kdterm_topk_kernel(tc, qT, k_words, k_scales, t, ls, offs, out):
         psum = ctx.enter_context(tc.psum_pool(name="psum", bufs=1))
 
         offsets = keep.tile([P, SLOTS // 16], U16, name="offsets")
-        q_raw = keep.tile([P, PACK, NQ], F32, name="q_raw", tag="q_then_t")
+        q_raw = keep.tile([P, PACK, NQ], F32, name="q_raw")
         q_bf = keep.tile([P, NQ, PACK], BF16, name="q_bf", align_bytes=64)
         q_codes = keep.tile([P, NQ], U32, name="q_codes", align_bytes=64)
         q_scales = keep.tile([P, NQ], U8, name="q_scales", align_bytes=64)
         pool_words = keep.tile([P, VOCAB], I32, name="pool_words", align_bytes=64)
         zeros = pool_words[:, VOCAB - SLOTS // 4 :]
-        pool_scales = keep.tile([P, VOCAB], U8, name="pool_scales", tag="scales_then_ls", align_bytes=64)
+        pool_scales = keep.tile([P, VOCAB], U8, name="pool_scales", tag="scales_then_t", align_bytes=64)
         picked_scales = keep.tile([P, SLOTS], U8, name="picked_scales", align_bytes=64)
         key_scales = keep.tile([P, SLOTS], U8, name="key_scales", align_bytes=64)
         ln_t = keep.tile([P, SLOTS], F32, name="ln_t")
 
+        ls_rows = keep.tile([P, 32], F32, name="ls_rows", align_bytes=64)
+        ls_cols = keep.tile([P, 32], F32, name="ls_cols", align_bytes=64)
+        ls_sb = ls_cols[:, 0:1]
+
+        nc.vector.memset(ls_rows[:], 0.0)
         nc.vector.memset(zeros, 0)
         nc.vector.memset(pool_scales[:].bitcast(I32), 0)
         nc.vector.tensor_copy(out=key_scales[:].bitcast(I32), in_=zeros)
@@ -54,9 +59,10 @@ def tile_attend_kdterm_topk_kernel(tc, qT, k_words, k_scales, t, ls, offs, out):
         nc.sync.dma_start(out=pool_scales[:].bitcast(I32)[11 : 11 + 7 * 15 + 1 : 7, :], in_=k_scales[0].bitcast(I32))
         nc.sync.dma_start(out=pool_words[:, HEAD:], in_=words[:, HEAD:])
 
+        nc.scalar.dma_start(out=ls_rows[0:P:32, :], in_=ls[0].rearrange("(b i) o -> b (i o)", i=32))
+        nc.vector.transpose(out=ls_cols[:], in_=ls_rows[:])
+
         nc.vector.tensor_copy(out=q_bf[:], in_=q_raw[:].rearrange("p j w -> p w j"))
-        t_sb = keep.tile([P, SLOTS], F32, name="t_sb", tag="q_then_t")
-        nc.sync.dma_start(out=t_sb[:], in_=t[0])
 
         nc.vector.tensor_copy(picked_scales[:], pool_scales[:].indirect(offsets[:]))
         for j in range(4):
@@ -64,8 +70,8 @@ def tile_attend_kdterm_topk_kernel(tc, qT, k_words, k_scales, t, ls, offs, out):
                 out=key_scales[:].bitcast(I32)[j:P:32, :], in_=picked_scales[:].bitcast(I32)[11 + 7 * j : 11 + 7 * (12 + j) + 1 : 28, :]
             )
 
-        ls_sb = keep.tile([P, 1], F32, name="ls_sb", tag="scales_then_ls", align_bytes=64)
-        nc.sync.dma_start(out=ls_sb[:], in_=ls[0])
+        t_sb = keep.tile([P, SLOTS], F32, name="t_sb", tag="scales_then_t", align_bytes=64)
+        nc.sync.dma_start(out=t_sb[:], in_=t[0])
 
         nc.vector.quantize_mx(
             out=q_codes[:].bitcast(FP8X4),
@@ -95,15 +101,13 @@ def tile_attend_kdterm_topk_kernel(tc, qT, k_words, k_scales, t, ls, offs, out):
             )
             diffs[h] = keep.tile([P, PIECE], F32, name="diff%d" % h)
             nc.vector.scalar_tensor_tensor(
-                out=diffs[h][:], in0=acc[:], scalar=ls_sb[:], in1=ln_t[:, cols], op0=ALU.subtract, op1=ALU.subtract
+                out=diffs[h][:], in0=ln_t[:, cols], scalar=ls_sb, in1=acc[:], op0=ALU.add, op1=ALU.subtract
             )
 
         def weigh(h):
             cols = slice(h * PIECE, (h + 1) * PIECE)
             y = keep.tile([P, PIECE], F32, name="y%d" % h)
-            nc.vector.scalar_tensor_tensor(
-                out=y[:], in0=diffs[h][:], scalar=-1.0, in1=t_sb[:, cols], op0=ALU.mult, op1=ALU.mult
-            )
+            nc.vector.tensor_tensor(out=y[:], in0=diffs[h][:], in1=t_sb[:, cols], op=ALU.mult)
             queue = nc.scalar if h % 2 == 0 else nc.sync
             queue.dma_start(out=out[0][:, cols], in_=y[:])
 

@@ -18,7 +18,7 @@ NQ = 128
 SLOTS = 512
 VOCAB = 4096
 D = 512
-HEAD = 640
+CUTS = (0, 1024, 2048, VOCAB)
 PIECES = 4
 PIECE = SLOTS // PIECES
 
@@ -37,8 +37,7 @@ def tile_attend_kdterm_topk_kernel(tc, qT, k_words, k_scales, t, ls, offs, out):
         q_codes = keep.tile([P, NQ], U32, name="q_codes", align_bytes=64)
         q_scales = keep.tile([P, NQ], U8, name="q_scales", align_bytes=64)
         pool_words = keep.tile([P, VOCAB], I32, name="pool_words", align_bytes=64)
-        zeros = pool_words[:, VOCAB - SLOTS // 4 :]
-        pool_scales = keep.tile([P, VOCAB], U8, name="pool_scales", tag="scales_then_t", align_bytes=64)
+        pool_scales = keep.tile([P, VOCAB], U8, name="pool_scales", tag="scales_then_keys", align_bytes=64)
         picked_scales = keep.tile([P, SLOTS], U8, name="picked_scales", align_bytes=64)
         key_scales = keep.tile([P, SLOTS], U8, name="key_scales", align_bytes=64)
         ln_t = keep.tile([P, SLOTS], F32, name="ln_t")
@@ -47,19 +46,19 @@ def tile_attend_kdterm_topk_kernel(tc, qT, k_words, k_scales, t, ls, offs, out):
         ls_cols = keep.tile([P, 32], F32, name="ls_cols", align_bytes=64)
         ls_sb = ls_cols[:, 0:1]
 
-        nc.vector.memset(ls_rows[:], 0.0)
-        nc.vector.memset(zeros, 0)
         nc.vector.memset(pool_scales[:].bitcast(I32), 0)
-        nc.vector.tensor_copy(out=key_scales[:].bitcast(I32), in_=zeros)
+        nc.vector.memset(ls_rows[:], 0.0)
 
         nc.sync.dma_start(out=q_raw[:], in_=qT[0].rearrange("(p j) w -> p j w", j=PACK))
         nc.sync.dma_start(offsets[:], offs)
         words = k_words[0].rearrange("p n r -> p (n r)").bitcast(I32)
-        nc.sync.dma_start(out=pool_words[:, :HEAD], in_=words[:, :HEAD])
+        for a, b in zip(CUTS[:-1], CUTS[1:]):
+            nc.scalar.dma_start(out=pool_words[:, a:b], in_=words[:, a:b])
+        t_sb = keep.tile([P, SLOTS], F32, name="t_sb")
+        nc.scalar.dma_start(out=t_sb[:], in_=t[0])
         nc.sync.dma_start(out=pool_scales[:].bitcast(I32)[11 : 11 + 7 * 15 + 1 : 7, :], in_=k_scales[0].bitcast(I32))
-        nc.sync.dma_start(out=pool_words[:, HEAD:], in_=words[:, HEAD:])
 
-        nc.scalar.dma_start(out=ls_rows[0:P:32, :], in_=ls[0].rearrange("(b i) o -> b (i o)", i=32))
+        nc.sync.dma_start(out=ls_rows[0:P:32, :], in_=ls[0].rearrange("(b i) o -> b (i o)", i=32))
         nc.vector.transpose(out=ls_cols[:], in_=ls_rows[:])
 
         nc.vector.tensor_copy(out=q_bf[:], in_=q_raw[:].rearrange("p j w -> p w j"))
@@ -70,15 +69,13 @@ def tile_attend_kdterm_topk_kernel(tc, qT, k_words, k_scales, t, ls, offs, out):
                 out=key_scales[:].bitcast(I32)[j:P:32, :], in_=picked_scales[:].bitcast(I32)[11 + 7 * j : 11 + 7 * (12 + j) + 1 : 28, :]
             )
 
-        t_sb = keep.tile([P, SLOTS], F32, name="t_sb", tag="scales_then_t", align_bytes=64)
-        nc.sync.dma_start(out=t_sb[:], in_=t[0])
 
         nc.vector.quantize_mx(
             out=q_codes[:].bitcast(FP8X4),
             scales=q_scales[:],
             in_=q_bf[:].rearrange("p w j -> p (w j)"),
         )
-        key_words = keep.tile([P, SLOTS], U32, name="key_words", align_bytes=64)
+        key_words = keep.tile([P, SLOTS], U32, name="key_words", tag="scales_then_keys", align_bytes=64)
         nc.vector.tensor_copy(key_words[:], pool_words[:].bitcast(U32).indirect(offsets[:]))
 
         for half in range(2):

@@ -18,7 +18,7 @@ NQ = 128
 SLOTS = 512
 VOCAB = 4096
 D = 512
-CUTS = (0, 1024, 2048, VOCAB)
+HEAD = 1344
 PIECES = 4
 PIECE = SLOTS // PIECES
 
@@ -29,54 +29,62 @@ def tile_attend_kdterm_topk_kernel(tc, qT, k_words, k_scales, t, ls, offs, out):
     nc = tc.nc
     with ExitStack() as ctx:
         keep = ctx.enter_context(tc.tile_pool(name="keep", bufs=1))
+        shared = ctx.enter_context(tc.tile_pool(name="shared", bufs=1))
         psum = ctx.enter_context(tc.psum_pool(name="psum", bufs=1))
 
         offsets = keep.tile([P, SLOTS // 16], U16, name="offsets")
-        q_raw = keep.tile([P, PACK, NQ], F32, name="q_raw")
+        ls_rows = shared.tile([P, 32], F32, name="ls_rows", align_bytes=64, offset=20480)
         q_bf = keep.tile([P, NQ, PACK], BF16, name="q_bf", align_bytes=64)
-        q_codes = keep.tile([P, NQ], U32, name="q_codes", align_bytes=64)
-        q_scales = keep.tile([P, NQ], U8, name="q_scales", align_bytes=64)
-        pool_words = keep.tile([P, VOCAB], I32, name="pool_words", align_bytes=64)
-        pool_scales = keep.tile([P, VOCAB], U8, name="pool_scales", tag="scales_then_keys", align_bytes=64)
+        pool_words = shared.tile([P, VOCAB], I32, name="pool_words", align_bytes=64, offset=4096)
+        zeros = pool_words[:, VOCAB - SLOTS // 4 :]
+        pool_scales = shared.tile([P, VOCAB], U8, name="pool_scales", align_bytes=64, offset=0)
         picked_scales = keep.tile([P, SLOTS], U8, name="picked_scales", align_bytes=64)
         key_scales = keep.tile([P, SLOTS], U8, name="key_scales", align_bytes=64)
         ln_t = keep.tile([P, SLOTS], F32, name="ln_t")
 
-        ls_rows = keep.tile([P, 32], F32, name="ls_rows", align_bytes=64)
-        ls_cols = keep.tile([P, 32], F32, name="ls_cols", align_bytes=64)
-        ls_sb = ls_cols[:, 0:1]
-
+        nc.gpsimd.memset(ls_rows[:], 0.0)
+        nc.vector.memset(zeros, 0)
         nc.vector.memset(pool_scales[:].bitcast(I32), 0)
-        nc.vector.memset(ls_rows[:], 0.0)
+        nc.vector.tensor_copy(out=key_scales[:].bitcast(I32), in_=zeros)
+        one = keep.tile([P, 1], F32, name="one")
+        unread = keep.tile([P, 1], F32, name="unread")
+        nc.gpsimd.memset(one[:], 1.0)
 
-        nc.sync.dma_start(out=q_raw[:], in_=qT[0].rearrange("(p j) w -> p j w", j=PACK))
         nc.sync.dma_start(offsets[:], offs)
         words = k_words[0].rearrange("p n r -> p (n r)").bitcast(I32)
-        for a, b in zip(CUTS[:-1], CUTS[1:]):
-            nc.scalar.dma_start(out=pool_words[:, a:b], in_=words[:, a:b])
-        t_sb = keep.tile([P, SLOTS], F32, name="t_sb")
-        nc.scalar.dma_start(out=t_sb[:], in_=t[0])
-        nc.sync.dma_start(out=pool_scales[:].bitcast(I32)[11 : 11 + 7 * 15 + 1 : 7, :], in_=k_scales[0].bitcast(I32))
-
+        nc.sync.dma_start(out=pool_words[:, :HEAD], in_=words[:, :HEAD])
         nc.sync.dma_start(out=ls_rows[0:P:32, :], in_=ls[0].rearrange("(b i) o -> b (i o)", i=32))
-        nc.vector.transpose(out=ls_cols[:], in_=ls_rows[:])
+        nc.sync.dma_start(out=pool_scales[:].bitcast(I32)[11 : 11 + 7 * 15 + 1 : 7, :], in_=k_scales[0].bitcast(I32))
+        nc.sync.dma_start(out=pool_words[:, HEAD:], in_=words[:, HEAD:])
 
-        nc.vector.tensor_copy(out=q_bf[:], in_=q_raw[:].rearrange("p j w -> p w j"))
+        ls_cols = keep.tile([P, 32], F32, name="ls_cols", align_bytes=64)
+        ls_sb = ls_cols[:, 0:1]
+        nc.vector.transpose(out=ls_cols[:], in_=ls_rows[:])
+        q_raw = shared.tile([P, PACK, NQ], F32, name="q_raw", align_bytes=64, offset=20480)
+        nc.sync.dma_start(out=q_raw[:], in_=qT[0].rearrange("(p j) w -> p j w", j=PACK))
+
+        nc.scalar.activation(out=unread[:], in_=one[:], func=ACT.Ln)
+        nc.scalar.copy(
+            out=q_bf[:].rearrange("p (c i) j -> p c j i", i=4), in_=q_raw[:].rearrange("p j (c i) -> p c j i", i=4)
+        )
 
         nc.vector.tensor_copy(picked_scales[:], pool_scales[:].indirect(offsets[:]))
+        t_sb = shared.tile([P, SLOTS], F32, name="t_sb", align_bytes=64, offset=2048)
+        nc.sync.dma_start(out=t_sb[:], in_=t[0])
         for j in range(4):
             nc.sync.dma_start(
                 out=key_scales[:].bitcast(I32)[j:P:32, :], in_=picked_scales[:].bitcast(I32)[11 + 7 * j : 11 + 7 * (12 + j) + 1 : 28, :]
             )
 
-
+        key_words = shared.tile([P, SLOTS], U32, name="key_words", align_bytes=64, offset=0)
+        nc.vector.tensor_copy(key_words[:], pool_words[:].bitcast(U32).indirect(offsets[:]))
+        q_codes = shared.tile([P, NQ], U32, name="q_codes", align_bytes=64, offset=4096)
+        q_scales = shared.tile([P, NQ], U8, name="q_scales", align_bytes=64, offset=4096 + 512)
         nc.vector.quantize_mx(
             out=q_codes[:].bitcast(FP8X4),
             scales=q_scales[:],
             in_=q_bf[:].rearrange("p w j -> p (w j)"),
         )
-        key_words = keep.tile([P, SLOTS], U32, name="key_words", tag="scales_then_keys", align_bytes=64)
-        nc.vector.tensor_copy(key_words[:], pool_words[:].bitcast(U32).indirect(offsets[:]))
 
         for half in range(2):
             cols = slice(half * SLOTS // 2, (half + 1) * SLOTS // 2)

@@ -33,9 +33,9 @@ def tile_attend_kdterm_topk_kernel(tc, qT, k_words, k_scales, t, ls, offs, out):
         psum = ctx.enter_context(tc.psum_pool(name="psum", bufs=1))
 
         offsets = keep.tile([P, SLOTS // 16], U16, name="offsets")
-        ls_rows = shared.tile([P, 32], F32, name="ls_rows", align_bytes=64, offset=20480)
+        ls_rows = shared.tile([P, 40], F32, name="ls_rows", align_bytes=64, offset=5120 - 64)
         q_bf = keep.tile([P, NQ, PACK], BF16, name="q_bf", align_bytes=64)
-        pool_words = shared.tile([P, VOCAB], I32, name="pool_words", align_bytes=64, offset=4096)
+        pool_words = keep.tile([P, VOCAB], I32, name="pool_words", align_bytes=64)
         zeros = pool_words[:, VOCAB - SLOTS // 4 :]
         pool_scales = shared.tile([P, VOCAB], U8, name="pool_scales", align_bytes=64, offset=0)
         picked_scales = keep.tile([P, SLOTS], U8, name="picked_scales", align_bytes=64)
@@ -46,48 +46,48 @@ def tile_attend_kdterm_topk_kernel(tc, qT, k_words, k_scales, t, ls, offs, out):
         nc.vector.memset(zeros, 0)
         nc.vector.memset(pool_scales[:].bitcast(I32), 0)
         nc.vector.tensor_copy(out=key_scales[:].bitcast(I32), in_=zeros)
-        one = keep.tile([P, 1], F32, name="one")
         unread = keep.tile([P, 1], F32, name="unread")
-        nc.gpsimd.memset(one[:], 1.0)
 
         nc.sync.dma_start(offsets[:], offs)
         words = k_words[0].rearrange("p n r -> p (n r)").bitcast(I32)
         nc.sync.dma_start(out=pool_words[:, :HEAD], in_=words[:, :HEAD])
-        nc.sync.dma_start(out=ls_rows[0:P:32, :], in_=ls[0].rearrange("(b i) o -> b (i o)", i=32))
+        nc.sync.dma_start(out=ls_rows[0:P:32, :32], in_=ls[0].rearrange("(b i) o -> b (i o)", i=32))
         nc.sync.dma_start(out=pool_scales[:].bitcast(I32)[11 : 11 + 7 * 15 + 1 : 7, :], in_=k_scales[0].bitcast(I32))
         nc.sync.dma_start(out=pool_words[:, HEAD:], in_=words[:, HEAD:])
 
         ls_cols = keep.tile([P, 32], F32, name="ls_cols", align_bytes=64)
         ls_sb = ls_cols[:, 0:1]
-        nc.vector.transpose(out=ls_cols[:], in_=ls_rows[:])
-        q_raw = shared.tile([P, PACK, NQ], F32, name="q_raw", align_bytes=64, offset=20480)
-        nc.sync.dma_start(out=q_raw[:], in_=qT[0].rearrange("(p j) w -> p j w", j=PACK))
+        nc.vector.transpose(out=ls_cols[:], in_=ls_rows[:, :32])
 
-        nc.scalar.activation(out=unread[:], in_=one[:], func=ACT.Ln)
-        nc.scalar.copy(
-            out=q_bf[:].rearrange("p (c i) j -> p c j i", i=4), in_=q_raw[:].rearrange("p j (c i) -> p c j i", i=4)
-        )
+        nc.scalar.activation(out=unread[:], in_=ls_rows[:, 32:33], func=ACT.Ln, bias=1.0)
+
+        q_rows = qT[0].rearrange("(p j) w -> p j w", j=PACK)
+        for u in range(2):
+            q_raw = shared.tile([P, 2, NQ], F32, name="q_raw%d" % u, align_bytes=64, offset=4096 + 1024 * u)
+            nc.sync.dma_start(out=q_raw[:], in_=q_rows[:, 2 * u : 2 * u + 2, :])
+            nc.scalar.copy(out=q_bf[:, :, 2 * u : 2 * u + 2], in_=q_raw[:].rearrange("p j w -> p w j"))
 
         nc.vector.tensor_copy(picked_scales[:], pool_scales[:].indirect(offsets[:]))
-        t_sb = shared.tile([P, SLOTS], F32, name="t_sb", align_bytes=64, offset=2048)
-        nc.sync.dma_start(out=t_sb[:], in_=t[0])
         for j in range(4):
-            nc.sync.dma_start(
+            queue = nc.scalar if j % 2 == 0 else nc.sync
+            queue.dma_start(
                 out=key_scales[:].bitcast(I32)[j:P:32, :], in_=picked_scales[:].bitcast(I32)[11 + 7 * j : 11 + 7 * (12 + j) + 1 : 28, :]
             )
+        t_sb = shared.tile([P, SLOTS], F32, name="t_sb", align_bytes=64, offset=2048)
+        nc.sync.dma_start(out=t_sb[:], in_=t[0])
 
         key_words = shared.tile([P, SLOTS], U32, name="key_words", align_bytes=64, offset=0)
         nc.vector.tensor_copy(key_words[:], pool_words[:].bitcast(U32).indirect(offsets[:]))
-        q_codes = shared.tile([P, NQ], U32, name="q_codes", align_bytes=64, offset=4096)
-        q_scales = shared.tile([P, NQ], U8, name="q_scales", align_bytes=64, offset=4096 + 512)
+        q_codes = keep.tile([P, NQ], U32, name="q_codes", align_bytes=64)
+        q_scales = keep.tile([P, NQ], U8, name="q_scales", align_bytes=64)
         nc.vector.quantize_mx(
             out=q_codes[:].bitcast(FP8X4),
             scales=q_scales[:],
             in_=q_bf[:].rearrange("p w j -> p (w j)"),
         )
 
-        for half in range(2):
-            cols = slice(half * SLOTS // 2, (half + 1) * SLOTS // 2)
+        for h in range(PIECES):
+            cols = slice(h * PIECE, (h + 1) * PIECE)
             nc.scalar.activation(out=ln_t[:, cols], in_=t_sb[:, cols], func=ACT.Ln)
 
         diffs = {}

@@ -19,6 +19,7 @@ SLOTS = 512
 VOCAB = 4096
 D = 512
 HEAD = 1344
+SPLIT = 80
 PIECES = 4
 PIECE = SLOTS // PIECES
 
@@ -62,10 +63,20 @@ def tile_attend_kdterm_topk_kernel(tc, qT, k_words, k_scales, t, ls, offs, out):
         nc.scalar.activation(out=unread[:], in_=ls_rows[:, 32:33], func=ACT.Ln, bias=1.0)
 
         q_rows = qT[0].rearrange("(p j) w -> p j w", j=PACK)
-        for u in range(2):
-            q_raw = shared.tile([P, 2, NQ], F32, name="q_raw%d" % u, align_bytes=64, offset=4096 + 1024 * u)
-            nc.sync.dma_start(out=q_raw[:], in_=q_rows[:, 2 * u : 2 * u + 2, :])
-            nc.scalar.copy(out=q_bf[:, :, 2 * u : 2 * u + 2], in_=q_raw[:].rearrange("p j w -> p w j"))
+        q_raw = shared.tile([P, PACK, NQ], F32, name="q_raw", align_bytes=64, offset=4096)
+        nc.sync.dma_start(out=q_raw[:], in_=q_rows)
+        nc.scalar.copy(
+            out=q_bf[:, :SPLIT, :].rearrange("p (c i) j -> p c j i", i=4),
+            in_=q_raw[:, :, :SPLIT].rearrange("p j (c i) -> p c j i", i=4),
+        )
+        nc.gpsimd.tensor_scalar(
+            out=q_bf[:, SPLIT:, :],
+            in0=q_raw[:, :, SPLIT:].rearrange("p j w -> p w j"),
+            scalar1=1.0,
+            scalar2=0.0,
+            op0=ALU.mult,
+            op1=ALU.add,
+        )
 
         nc.vector.tensor_copy(picked_scales[:], pool_scales[:].indirect(offsets[:]))
         for j in range(4):

@@ -34,7 +34,7 @@ def tile_attend_kdterm_topk_kernel(tc, qT, k_words, k_scales, t, ls, offs, out):
         psum = ctx.enter_context(tc.psum_pool(name="psum", bufs=1))
 
         offsets = keep.tile([P, SLOTS // 16], U16, name="offsets")
-        ls_rows = shared.tile([P, 40], F32, name="ls_rows", align_bytes=64, offset=5120 - 64)
+        ls_rows = shared.tile([P, 40], F32, name="ls_rows", align_bytes=64, offset=6144 - 64)
         q_bf = keep.tile([P, NQ, PACK], BF16, name="q_bf", align_bytes=64)
         pool_words = keep.tile([P, VOCAB], I32, name="pool_words", align_bytes=64)
         zeros = pool_words[:, VOCAB - SLOTS // 4 :]
@@ -43,7 +43,9 @@ def tile_attend_kdterm_topk_kernel(tc, qT, k_words, k_scales, t, ls, offs, out):
         key_scales = keep.tile([P, SLOTS], U8, name="key_scales", align_bytes=64)
         ln_t = keep.tile([P, SLOTS], F32, name="ln_t")
 
+        y = keep.tile([P, SLOTS], F32, name="y")
         nc.gpsimd.memset(ls_rows[:], 0.0)
+        nc.gpsimd.memset(y[:, PIECE - 1 : PIECE + 1], 0.0)
         nc.vector.memset(zeros, 0)
         nc.vector.memset(pool_scales[:].bitcast(I32), 0)
         nc.vector.tensor_copy(out=key_scales[:].bitcast(I32), in_=zeros)
@@ -78,14 +80,21 @@ def tile_attend_kdterm_topk_kernel(tc, qT, k_words, k_scales, t, ls, offs, out):
             op1=ALU.add,
         )
 
+        t_half = [
+            shared.tile([P, SLOTS // 2], F32, name="t_half0", align_bytes=64, offset=6144),
+            shared.tile([P, SLOTS // 2], F32, name="t_half1", align_bytes=64, offset=2048),
+        ]
+        nc.sync.dma_start(out=t_half[0][:], in_=t[0][:, : SLOTS // 2])
+
+        def t_piece(h):
+            return t_half[h // 2][:, (h % 2) * PIECE : (h % 2 + 1) * PIECE]
+
         nc.vector.tensor_copy(picked_scales[:], pool_scales[:].indirect(offsets[:]))
         for j in range(4):
-            queue = nc.scalar if j % 2 == 0 else nc.sync
-            queue.dma_start(
+            nc.sync.dma_start(
                 out=key_scales[:].bitcast(I32)[j:P:32, :], in_=picked_scales[:].bitcast(I32)[11 + 7 * j : 11 + 7 * (12 + j) + 1 : 28, :]
             )
-        t_sb = shared.tile([P, SLOTS], F32, name="t_sb", align_bytes=64, offset=2048)
-        nc.sync.dma_start(out=t_sb[:], in_=t[0])
+        nc.sync.dma_start(out=t_half[1][:], in_=t[0][:, SLOTS // 2 :])
 
         key_words = shared.tile([P, SLOTS], U32, name="key_words", align_bytes=64, offset=0)
         nc.vector.tensor_copy(key_words[:], pool_words[:].bitcast(U32).indirect(offsets[:]))
@@ -99,7 +108,8 @@ def tile_attend_kdterm_topk_kernel(tc, qT, k_words, k_scales, t, ls, offs, out):
 
         for h in range(PIECES):
             cols = slice(h * PIECE, (h + 1) * PIECE)
-            nc.scalar.activation(out=ln_t[:, cols], in_=t_sb[:, cols], func=ACT.Ln)
+            bias = y[:, PIECE + h - 3 : PIECE + h - 2] if h >= 2 else 0.0
+            nc.scalar.activation(out=ln_t[:, cols], in_=t_piece(h), func=ACT.Ln, bias=bias)
 
         diffs = {}
 
@@ -122,10 +132,9 @@ def tile_attend_kdterm_topk_kernel(tc, qT, k_words, k_scales, t, ls, offs, out):
 
         def weigh(h):
             cols = slice(h * PIECE, (h + 1) * PIECE)
-            y = keep.tile([P, PIECE], F32, name="y%d" % h)
-            nc.vector.tensor_tensor(out=y[:], in0=diffs[h][:], in1=t_sb[:, cols], op=ALU.mult)
+            nc.vector.tensor_tensor(out=y[:, cols], in0=diffs[h][:], in1=t_piece(h), op=ALU.mult)
             queue = nc.scalar if h % 2 == 0 else nc.sync
-            queue.dma_start(out=out[0][:, cols], in_=y[:])
+            queue.dma_start(out=out[0][:, cols], in_=y[:, cols])
 
         LAG = 2
         for h in range(PIECES + LAG):

@@ -18,8 +18,9 @@ NQ = 128
 SLOTS = 512
 VOCAB = 4096
 D = 512
-HEAD = 1344
-SPLIT = 80
+HEAD = 1408
+HALF = NQ // 2
+SPLIT = 100
 PIECES = 4
 PIECE = SLOTS // PIECES
 
@@ -51,9 +52,9 @@ def tile_attend_kdterm_topk_kernel(tc, qT, k_words, k_scales, t, ls, offs, out):
         nc.vector.tensor_copy(out=key_scales[:].bitcast(I32), in_=zeros)
         unread = keep.tile([P, 1], F32, name="unread")
 
-        nc.sync.dma_start(offsets[:], offs)
         words = k_words[0].rearrange("p n r -> p (n r)").bitcast(I32)
         nc.sync.dma_start(out=pool_words[:, :HEAD], in_=words[:, :HEAD])
+        nc.sync.dma_start(offsets[:], offs)
         nc.sync.dma_start(out=ls_rows[0:P:32, :32], in_=ls[0].rearrange("(b i) o -> b (i o)", i=32))
         nc.sync.dma_start(out=pool_scales[:].bitcast(I32)[11 : 11 + 7 * 15 + 1 : 7, :], in_=k_scales[0].bitcast(I32))
         nc.sync.dma_start(out=pool_words[:, HEAD:], in_=words[:, HEAD:])
@@ -67,10 +68,11 @@ def tile_attend_kdterm_topk_kernel(tc, qT, k_words, k_scales, t, ls, offs, out):
         q_rows = qT[0].rearrange("(p j) w -> p j w", j=PACK)
         q_raw = shared.tile([P, PACK, NQ], F32, name="q_raw", align_bytes=64, offset=4096)
         nc.sync.dma_start(out=q_raw[:], in_=q_rows)
-        nc.scalar.copy(
-            out=q_bf[:, :SPLIT, :].rearrange("p (c i) j -> p c j i", i=4),
-            in_=q_raw[:, :, :SPLIT].rearrange("p j (c i) -> p c j i", i=4),
-        )
+        for queries in (slice(0, HALF), slice(HALF, SPLIT)):
+            nc.scalar.copy(
+                out=q_bf[:, queries, :].rearrange("p (c i) j -> p c j i", i=4),
+                in_=q_raw[:, :, queries].rearrange("p j (c i) -> p c j i", i=4),
+            )
         nc.gpsimd.tensor_scalar(
             out=q_bf[:, SPLIT:, :],
             in0=q_raw[:, :, SPLIT:].rearrange("p j w -> p w j"),
@@ -100,11 +102,13 @@ def tile_attend_kdterm_topk_kernel(tc, qT, k_words, k_scales, t, ls, offs, out):
         nc.vector.tensor_copy(key_words[:], pool_words[:].bitcast(U32).indirect(offsets[:]))
         q_codes = keep.tile([P, NQ], U32, name="q_codes", align_bytes=64)
         q_scales = keep.tile([P, NQ], U8, name="q_scales", align_bytes=64)
-        nc.vector.quantize_mx(
-            out=q_codes[:].bitcast(FP8X4),
-            scales=q_scales[:],
-            in_=q_bf[:].rearrange("p w j -> p (w j)"),
-        )
+        for u in range(2):
+            half = slice(u * HALF, (u + 1) * HALF)
+            nc.vector.quantize_mx(
+                out=q_codes[:, half].bitcast(FP8X4),
+                scales=q_scales[:, half],
+                in_=q_bf[:, half, :].rearrange("p w j -> p (w j)"),
+            )
 
         for h in range(PIECES):
             cols = slice(h * PIECE, (h + 1) * PIECE)

@@ -43,6 +43,7 @@ def tile_attend_kdterm_topk_kernel(tc, qT, k_words, k_scales, t, ls, offs, out):
         picked_scales = keep.tile([P, SLOTS], U8, name="picked_scales", align_bytes=64)
         key_scales = keep.tile([P, SLOTS], U8, name="key_scales", align_bytes=64)
         ln_t = keep.tile([P, SLOTS], F32, name="ln_t")
+        ln_ls = keep.tile([P, SLOTS // 2], F32, name="ln_ls")
 
         y = keep.tile([P, SLOTS], F32, name="y")
         nc.gpsimd.memset(ls_rows[:], 0.0)
@@ -115,6 +116,9 @@ def tile_attend_kdterm_topk_kernel(tc, qT, k_words, k_scales, t, ls, offs, out):
             bias = y[:, PIECE + h - 3 : PIECE + h - 2] if h >= 2 else 0.0
             nc.scalar.activation(out=ln_t[:, cols], in_=t_piece(h), func=ACT.Ln, bias=bias)
 
+            if h < PIECES // 2:
+                nc.scalar.activation(out=ln_ls[:, cols], in_=ln_t[:, cols], func=ACT.Identity, bias=ls_sb)
+
         diffs = {}
 
         def subtract(h):
@@ -130,9 +134,12 @@ def tile_attend_kdterm_topk_kernel(tc, qT, k_words, k_scales, t, ls, offs, out):
                 stop=True,
             )
             diffs[h] = keep.tile([P, PIECE], F32, name="diff%d" % h)
-            nc.vector.scalar_tensor_tensor(
-                out=diffs[h][:], in0=ln_t[:, cols], scalar=ls_sb, in1=acc[:], op0=ALU.add, op1=ALU.subtract
-            )
+            if h < PIECES // 2:
+                nc.vector.tensor_tensor(out=diffs[h][:], in0=ln_ls[:, cols], in1=acc[:], op=ALU.subtract)
+            else:
+                nc.vector.scalar_tensor_tensor(
+                    out=diffs[h][:], in0=ln_t[:, cols], scalar=ls_sb, in1=acc[:], op0=ALU.add, op1=ALU.subtract
+                )
 
         def weigh(h):
             cols = slice(h * PIECE, (h + 1) * PIECE)

@@ -43,11 +43,9 @@ def tile_attend_kdterm_topk_kernel(tc, qT, k_words, k_scales, t, ls, offs, out):
         picked_scales = keep.tile([P, SLOTS], U8, name="picked_scales", align_bytes=64)
         key_scales = keep.tile([P, SLOTS], U8, name="key_scales", align_bytes=64)
         ln_t = keep.tile([P, SLOTS], F32, name="ln_t")
-        ln_ls = keep.tile([P, SLOTS // 2], F32, name="ln_ls")
 
         y = keep.tile([P, SLOTS], F32, name="y")
         nc.gpsimd.memset(ls_rows[:], 0.0)
-        nc.gpsimd.memset(y[:, PIECE - 1 : PIECE + 1], 0.0)
         nc.vector.memset(zeros, 0)
         nc.vector.memset(pool_scales[:].bitcast(I32), 0)
         nc.vector.tensor_copy(out=key_scales[:].bitcast(I32), in_=zeros)
@@ -83,21 +81,15 @@ def tile_attend_kdterm_topk_kernel(tc, qT, k_words, k_scales, t, ls, offs, out):
             op1=ALU.add,
         )
 
-        t_half = [
-            shared.tile([P, SLOTS // 2], F32, name="t_half0", align_bytes=64, offset=6144),
-            shared.tile([P, SLOTS // 2], F32, name="t_half1", align_bytes=64, offset=2048),
-        ]
-        nc.sync.dma_start(out=t_half[0][:], in_=t[0][:, : SLOTS // 2])
-
-        def t_piece(h):
-            return t_half[h // 2][:, (h % 2) * PIECE : (h % 2 + 1) * PIECE]
+        t_sb = shared.tile([P, SLOTS], F32, name="t_sb", align_bytes=64, offset=6144)
+        nc.sync.dma_start(out=t_sb[:, : SLOTS // 2], in_=t[0][:, : SLOTS // 2])
+        nc.sync.dma_start(out=t_sb[:, SLOTS // 2 :], in_=t[0][:, SLOTS // 2 :])
 
         nc.vector.tensor_copy(picked_scales[:], pool_scales[:].indirect(offsets[:]))
         for j in range(4):
             nc.sync.dma_start(
                 out=key_scales[:].bitcast(I32)[j:P:32, :], in_=picked_scales[:].bitcast(I32)[11 + 7 * j : 11 + 7 * (12 + j) + 1 : 28, :]
             )
-        nc.sync.dma_start(out=t_half[1][:], in_=t[0][:, SLOTS // 2 :])
 
         key_words = shared.tile([P, SLOTS], U32, name="key_words", align_bytes=64, offset=0)
         nc.vector.tensor_copy(key_words[:], pool_words[:].bitcast(U32).indirect(offsets[:]))
@@ -111,13 +103,15 @@ def tile_attend_kdterm_topk_kernel(tc, qT, k_words, k_scales, t, ls, offs, out):
                 in_=q_bf[:, half, :].rearrange("p w j -> p (w j)"),
             )
 
-        for h in range(PIECES):
-            cols = slice(h * PIECE, (h + 1) * PIECE)
-            bias = y[:, PIECE + h - 3 : PIECE + h - 2] if h >= 2 else 0.0
-            nc.scalar.activation(out=ln_t[:, cols], in_=t_piece(h), func=ACT.Ln, bias=bias)
-
-            if h < PIECES // 2:
-                nc.scalar.activation(out=ln_ls[:, cols], in_=ln_t[:, cols], func=ACT.Identity, bias=ls_sb)
+        early = slice(0, SLOTS // 2)
+        late = slice(SLOTS // 2, SLOTS)
+        ahead = keep.tile([P, SLOTS], F32, name="ahead")
+        nc.scalar.activation(out=ln_t[:, early], in_=t_sb[:, early], func=ACT.Ln)
+        nc.scalar.activation(out=ln_t[:, late], in_=t_sb[:, late], func=ACT.Ln)
+        nc.vector.scalar_tensor_tensor(
+            out=ahead[:, early], in0=ln_t[:, early], scalar=ls_sb, in1=t_sb[:, early], op0=ALU.add, op1=ALU.mult
+        )
+        nc.vector.tensor_scalar(out=ahead[:, late], in0=ln_t[:, late], scalar1=ls_sb, scalar2=None, op0=ALU.add)
 
         diffs = {}
 
@@ -135,15 +129,16 @@ def tile_attend_kdterm_topk_kernel(tc, qT, k_words, k_scales, t, ls, offs, out):
             )
             diffs[h] = keep.tile([P, PIECE], F32, name="diff%d" % h)
             if h < PIECES // 2:
-                nc.vector.tensor_tensor(out=diffs[h][:], in0=ln_ls[:, cols], in1=acc[:], op=ALU.subtract)
+                nc.vector.tensor_tensor(out=diffs[h][:], in0=t_sb[:, cols], in1=acc[:], op=ALU.mult)
             else:
-                nc.vector.scalar_tensor_tensor(
-                    out=diffs[h][:], in0=ln_t[:, cols], scalar=ls_sb, in1=acc[:], op0=ALU.add, op1=ALU.subtract
-                )
+                nc.vector.tensor_tensor(out=diffs[h][:], in0=ahead[:, cols], in1=acc[:], op=ALU.subtract)
 
         def weigh(h):
             cols = slice(h * PIECE, (h + 1) * PIECE)
-            nc.vector.tensor_tensor(out=y[:, cols], in0=diffs[h][:], in1=t_piece(h), op=ALU.mult)
+            if h < PIECES // 2:
+                nc.vector.tensor_tensor(out=y[:, cols], in0=ahead[:, cols], in1=diffs[h][:], op=ALU.subtract)
+            else:
+                nc.vector.tensor_tensor(out=y[:, cols], in0=diffs[h][:], in1=t_sb[:, cols], op=ALU.mult)
             queue = nc.scalar if h % 2 == 0 else nc.sync
             queue.dma_start(out=out[0][:, cols], in_=y[:, cols])
 

@@ -20,7 +20,7 @@ VOCAB = 4096
 D = 512
 HEAD = 1408
 HALF = NQ // 2
-SPLIT = 100
+SPLIT = 88
 PIECES = 4
 PIECE = SLOTS // PIECES
 
@@ -67,14 +67,14 @@ def tile_attend_kdterm_topk_kernel(tc, qT, k_words, k_scales, t, ls, offs, out):
         q_rows = qT[0].rearrange("(p j) w -> p j w", j=PACK)
         q_raw = shared.tile([P, PACK, NQ], F32, name="q_raw", align_bytes=64, offset=4096)
         nc.sync.dma_start(out=q_raw[:], in_=q_rows)
-        for queries in (slice(0, HALF), slice(HALF, SPLIT)):
+        for queries in (slice(NQ - SPLIT, HALF), slice(HALF, NQ)):
             nc.scalar.copy(
                 out=q_bf[:, queries, :].rearrange("p (c i) j -> p c j i", i=4),
                 in_=q_raw[:, :, queries].rearrange("p j (c i) -> p c j i", i=4),
             )
         nc.gpsimd.tensor_scalar(
-            out=q_bf[:, SPLIT:, :],
-            in0=q_raw[:, :, SPLIT:].rearrange("p j w -> p w j"),
+            out=q_bf[:, : NQ - SPLIT, :],
+            in0=q_raw[:, :, : NQ - SPLIT].rearrange("p j w -> p w j"),
             scalar1=1.0,
             scalar2=0.0,
             op0=ALU.mult,

@@ -20,7 +20,7 @@ VOCAB = 4096
 D = 512
 HEAD = 1408
 HALF = NQ // 2
-SPLIT = 88
+SPLIT = 84
 PIECES = 4
 PIECE = SLOTS // PIECES
 
@@ -111,7 +111,8 @@ def tile_attend_kdterm_topk_kernel(tc, qT, k_words, k_scales, t, ls, offs, out):
         nc.vector.scalar_tensor_tensor(
             out=ahead[:, early], in0=ln_t[:, early], scalar=ls_sb, in1=t_sb[:, early], op0=ALU.add, op1=ALU.mult
         )
-        nc.vector.tensor_scalar(out=ahead[:, late], in0=ln_t[:, late], scalar1=ls_sb, scalar2=None, op0=ALU.add)
+        last = slice(SLOTS - PIECE, SLOTS)
+        nc.vector.tensor_scalar(out=ahead[:, last], in0=ln_t[:, last], scalar1=ls_sb, scalar2=None, op0=ALU.add)
 
         diffs = {}
 
@@ -130,6 +131,10 @@ def tile_attend_kdterm_topk_kernel(tc, qT, k_words, k_scales, t, ls, offs, out):
             diffs[h] = keep.tile([P, PIECE], F32, name="diff%d" % h)
             if h < PIECES // 2:
                 nc.vector.tensor_tensor(out=diffs[h][:], in0=t_sb[:, cols], in1=acc[:], op=ALU.mult)
+            elif h < PIECES - 1:
+                nc.vector.scalar_tensor_tensor(
+                    out=diffs[h][:], in0=ln_t[:, cols], scalar=ls_sb, in1=acc[:], op0=ALU.add, op1=ALU.subtract
+                )
             else:
                 nc.vector.tensor_tensor(out=diffs[h][:], in0=ahead[:, cols], in1=acc[:], op=ALU.subtract)
 

@@ -81,15 +81,21 @@ def tile_attend_kdterm_topk_kernel(tc, qT, k_words, k_scales, t, ls, offs, out):
             op1=ALU.add,
         )
 
-        t_sb = shared.tile([P, SLOTS], F32, name="t_sb", align_bytes=64, offset=6144)
-        nc.sync.dma_start(out=t_sb[:, : SLOTS // 2], in_=t[0][:, : SLOTS // 2])
-        nc.sync.dma_start(out=t_sb[:, SLOTS // 2 :], in_=t[0][:, SLOTS // 2 :])
+        t_early = shared.tile([P, SLOTS // 2], F32, name="t_early", align_bytes=64, offset=6144)
+        nc.sync.dma_start(out=t_early[:], in_=t[0][:, : SLOTS // 2])
 
         nc.vector.tensor_copy(picked_scales[:], pool_scales[:].indirect(offsets[:]))
+        t_late = shared.tile([P, SLOTS // 2], F32, name="t_late", align_bytes=64, offset=2048)
         for j in range(4):
+            if j == 2:
+                nc.sync.dma_start(out=t_late[:], in_=t[0][:, SLOTS // 2 :])
             nc.sync.dma_start(
                 out=key_scales[:].bitcast(I32)[j:P:32, :], in_=picked_scales[:].bitcast(I32)[11 + 7 * j : 11 + 7 * (12 + j) + 1 : 28, :]
             )
+
+        def t_piece(h):
+            half = t_early if h < PIECES // 2 else t_late
+            return half[:, (h % 2) * PIECE : (h % 2 + 1) * PIECE]
 
         key_words = shared.tile([P, SLOTS], U32, name="key_words", align_bytes=64, offset=0)
         nc.vector.tensor_copy(key_words[:], pool_words[:].bitcast(U32).indirect(offsets[:]))
@@ -106,10 +112,10 @@ def tile_attend_kdterm_topk_kernel(tc, qT, k_words, k_scales, t, ls, offs, out):
         early = slice(0, SLOTS // 2)
         late = slice(SLOTS // 2, SLOTS)
         ahead = keep.tile([P, SLOTS], F32, name="ahead")
-        nc.scalar.activation(out=ln_t[:, early], in_=t_sb[:, early], func=ACT.Ln)
-        nc.scalar.activation(out=ln_t[:, late], in_=t_sb[:, late], func=ACT.Ln)
+        nc.scalar.activation(out=ln_t[:, early], in_=t_early[:], func=ACT.Ln)
+        nc.scalar.activation(out=ln_t[:, late], in_=t_late[:], func=ACT.Ln)
         nc.vector.scalar_tensor_tensor(
-            out=ahead[:, early], in0=ln_t[:, early], scalar=ls_sb, in1=t_sb[:, early], op0=ALU.add, op1=ALU.mult
+            out=ahead[:, early], in0=ln_t[:, early], scalar=ls_sb, in1=t_early[:], op0=ALU.add, op1=ALU.mult
         )
         last = slice(SLOTS - PIECE, SLOTS)
         nc.vector.tensor_scalar(out=ahead[:, last], in0=ln_t[:, last], scalar1=ls_sb, scalar2=None, op0=ALU.add)
@@ -130,7 +136,7 @@ def tile_attend_kdterm_topk_kernel(tc, qT, k_words, k_scales, t, ls, offs, out):
             )
             diffs[h] = keep.tile([P, PIECE], F32, name="diff%d" % h)
             if h < PIECES // 2:
-                nc.vector.tensor_tensor(out=diffs[h][:], in0=t_sb[:, cols], in1=acc[:], op=ALU.mult)
+                nc.vector.tensor_tensor(out=diffs[h][:], in0=t_piece(h), in1=acc[:], op=ALU.mult)
             elif h < PIECES - 1:
                 nc.vector.scalar_tensor_tensor(
                     out=diffs[h][:], in0=ln_t[:, cols], scalar=ls_sb, in1=acc[:], op0=ALU.add, op1=ALU.subtract
@@ -143,7 +149,7 @@ def tile_attend_kdterm_topk_kernel(tc, qT, k_words, k_scales, t, ls, offs, out):
             if h < PIECES // 2:
                 nc.vector.tensor_tensor(out=y[:, cols], in0=ahead[:, cols], in1=diffs[h][:], op=ALU.subtract)
             else:
-                nc.vector.tensor_tensor(out=y[:, cols], in0=diffs[h][:], in1=t_sb[:, cols], op=ALU.mult)
+                nc.vector.tensor_tensor(out=y[:, cols], in0=diffs[h][:], in1=t_piece(h), op=ALU.mult)
             queue = nc.scalar if h % 2 == 0 else nc.sync
             queue.dma_start(out=out[0][:, cols], in_=y[:, cols])
 

@@ -18,7 +18,7 @@ NQ = 128
 SLOTS = 512
 VOCAB = 4096
 D = 512
-HEAD = 1408
+HEAD = 1024
 HALF = NQ // 2
 SPLIT = 84
 PIECES = 4

@@ -20,7 +20,7 @@ VOCAB = 4096
 D = 512
 HEAD = 1024
 HALF = NQ // 2
-SPLIT = 84
+SPLIT = 76
 PIECES = 4
 PIECE = SLOTS // PIECES
 
@@ -67,14 +67,14 @@ def tile_attend_kdterm_topk_kernel(tc, qT, k_words, k_scales, t, ls, offs, out):
         q_rows = qT[0].rearrange("(p j) w -> p j w", j=PACK)
         q_raw = shared.tile([P, PACK, NQ], F32, name="q_raw", align_bytes=64, offset=4096)
         nc.sync.dma_start(out=q_raw[:], in_=q_rows)
-        for queries in (slice(NQ - SPLIT, HALF), slice(HALF, NQ)):
+        for queries in (slice(0, HALF), slice(HALF, SPLIT)):
             nc.scalar.copy(
                 out=q_bf[:, queries, :].rearrange("p (c i) j -> p c j i", i=4),
                 in_=q_raw[:, :, queries].rearrange("p j (c i) -> p c j i", i=4),
             )
         nc.gpsimd.tensor_scalar(
-            out=q_bf[:, : NQ - SPLIT, :],
-            in0=q_raw[:, :, : NQ - SPLIT].rearrange("p j w -> p w j"),
+            out=q_bf[:, SPLIT:, :].rearrange("p (c i) j -> p c j i", i=4),
+            in0=q_raw[:, :, SPLIT:].rearrange("p j (c i) -> p c j i", i=4),
             scalar1=1.0,
             scalar2=0.0,
             op0=ALU.mult,

@@ -86,10 +86,10 @@ def tile_attend_kdterm_topk_kernel(tc, qT, k_words, k_scales, t, ls, offs, out):
 
         nc.vector.tensor_copy(picked_scales[:], pool_scales[:].indirect(offsets[:]))
         t_late = shared.tile([P, SLOTS // 2], F32, name="t_late", align_bytes=64, offset=2048)
+        nc.sync.dma_start(out=t_late[:], in_=t[0][:, SLOTS // 2 :])
         for j in range(4):
-            if j == 2:
-                nc.sync.dma_start(out=t_late[:], in_=t[0][:, SLOTS // 2 :])
-            nc.sync.dma_start(
+            queue = nc.scalar if j < 3 else nc.sync
+            queue.dma_start(
                 out=key_scales[:].bitcast(I32)[j:P:32, :], in_=picked_scales[:].bitcast(I32)[11 + 7 * j : 11 + 7 * (12 + j) + 1 : 28, :]
             )
 

from contextlib import ExitStack

import concourse.mybir as mybir

F32 = mybir.dt.float32
BF16 = mybir.dt.bfloat16
I32 = mybir.dt.int32
U32 = mybir.dt.uint32
U16 = mybir.dt.uint16
U8 = mybir.dt.uint8
FP8X4 = mybir.dt.float8_e4m3fn_x4
ALU = mybir.AluOpType
ACT = mybir.ActivationFunctionType

P = 128
PACK = 4
NQ = 128
SLOTS = 512
VOCAB = 4096
D = 512
HEAD = 1024
HALF = NQ // 2
SPLIT = 76
PIECES = 4
PIECE = SLOTS // PIECES

FLOPS = 2 * D * NQ * SLOTS


def tile_attend_kdterm_topk_kernel(tc, qT, k_words, k_scales, t, ls, offs, out):
    nc = tc.nc
    with ExitStack() as ctx:
        keep = ctx.enter_context(tc.tile_pool(name="keep", bufs=1))
        shared = ctx.enter_context(tc.tile_pool(name="shared", bufs=1))
        psum = ctx.enter_context(tc.psum_pool(name="psum", bufs=1))

        offsets = keep.tile([P, SLOTS // 16], U16, name="offsets")
        ls_rows = shared.tile([P, 40], F32, name="ls_rows", align_bytes=64, offset=6144 - 64)
        q_bf = keep.tile([P, NQ, PACK], BF16, name="q_bf", align_bytes=64)
        pool_words = keep.tile([P, VOCAB], I32, name="pool_words", align_bytes=64)
        zeros = pool_words[:, VOCAB - SLOTS // 4 :]
        pool_scales = shared.tile([P, VOCAB], U8, name="pool_scales", align_bytes=64, offset=0)
        picked_scales = keep.tile([P, SLOTS], U8, name="picked_scales", align_bytes=64)
        key_scales = keep.tile([P, SLOTS], U8, name="key_scales", align_bytes=64)
        ln_t = keep.tile([P, SLOTS], F32, name="ln_t")

        y = keep.tile([P, SLOTS], F32, name="y")
        nc.gpsimd.memset(ls_rows[:], 0.0)
        nc.vector.memset(zeros, 0)
        nc.vector.memset(pool_scales[:].bitcast(I32), 0)
        nc.vector.tensor_copy(out=key_scales[:].bitcast(I32), in_=zeros)
        unread = keep.tile([P, 1], F32, name="unread")

        words = k_words[0].rearrange("p n r -> p (n r)").bitcast(I32)
        nc.sync.dma_start(out=pool_words[:, :HEAD], in_=words[:, :HEAD])
        nc.sync.dma_start(offsets[:], offs)
        nc.sync.dma_start(out=ls_rows[0:P:32, :32], in_=ls[0].rearrange("(b i) o -> b (i o)", i=32))
        nc.sync.dma_start(out=pool_scales[:].bitcast(I32)[11 : 11 + 7 * 15 + 1 : 7, :], in_=k_scales[0].bitcast(I32))
        nc.sync.dma_start(out=pool_words[:, HEAD:], in_=words[:, HEAD:])

        ls_cols = keep.tile([P, 32], F32, name="ls_cols", align_bytes=64)
        ls_sb = ls_cols[:, 0:1]
        nc.vector.transpose(out=ls_cols[:], in_=ls_rows[:, :32])

        nc.scalar.activation(out=unread[:], in_=ls_rows[:, 32:33], func=ACT.Ln, bias=1.0)

        q_rows = qT[0].rearrange("(p j) w -> p j w", j=PACK)
        q_raw = shared.tile([P, PACK, NQ], F32, name="q_raw", align_bytes=64, offset=4096)
        nc.sync.dma_start(out=q_raw[:], in_=q_rows)
        for queries in (slice(0, HALF), slice(HALF, SPLIT)):
            nc.scalar.copy(
                out=q_bf[:, queries, :].rearrange("p (c i) j -> p c j i", i=4),
                in_=q_raw[:, :, queries].rearrange("p j (c i) -> p c j i", i=4),
            )
        nc.gpsimd.tensor_scalar(
            out=q_bf[:, SPLIT:, :].rearrange("p (c i) j -> p c j i", i=4),
            in0=q_raw[:, :, SPLIT:].rearrange("p j (c i) -> p c j i", i=4),
            scalar1=1.0,
            scalar2=0.0,
            op0=ALU.mult,
            op1=ALU.add,
        )

        t_early = shared.tile([P, SLOTS // 2], F32, name="t_early", align_bytes=64, offset=6144)
        nc.sync.dma_start(out=t_early[:], in_=t[0][:, : SLOTS // 2])

        nc.vector.tensor_copy(picked_scales[:], pool_scales[:].indirect(offsets[:]))
        t_late = shared.tile([P, SLOTS // 2], F32, name="t_late", align_bytes=64, offset=2048)
        nc.sync.dma_start(out=t_late[:], in_=t[0][:, SLOTS // 2 :])
        for j in range(4):
            queue = nc.scalar if j < 3 else nc.sync
            queue.dma_start(
                out=key_scales[:].bitcast(I32)[j:P:32, :], in_=picked_scales[:].bitcast(I32)[11 + 7 * j : 11 + 7 * (12 + j) + 1 : 28, :]
            )

        def t_piece(h):
            half = t_early if h < PIECES // 2 else t_late
            return half[:, (h % 2) * PIECE : (h % 2 + 1) * PIECE]

        key_words = shared.tile([P, SLOTS], U32, name="key_words", align_bytes=64, offset=0)
        nc.vector.tensor_copy(key_words[:], pool_words[:].bitcast(U32).indirect(offsets[:]))
        q_codes = keep.tile([P, NQ], U32, name="q_codes", align_bytes=64)
        q_scales = keep.tile([P, NQ], U8, name="q_scales", align_bytes=64)
        for u in range(2):
            half = slice(u * HALF, (u + 1) * HALF)
            nc.vector.quantize_mx(
                out=q_codes[:, half].bitcast(FP8X4),
                scales=q_scales[:, half],
                in_=q_bf[:, half, :].rearrange("p w j -> p (w j)"),
            )

        early = slice(0, SLOTS // 2)
        late = slice(SLOTS // 2, SLOTS)
        ahead = keep.tile([P, SLOTS], F32, name="ahead")
        nc.scalar.activation(out=ln_t[:, early], in_=t_early[:], func=ACT.Ln)
        nc.scalar.activation(out=ln_t[:, late], in_=t_late[:], func=ACT.Ln)
        nc.vector.scalar_tensor_tensor(
            out=ahead[:, early], in0=ln_t[:, early], scalar=ls_sb, in1=t_early[:], op0=ALU.add, op1=ALU.mult
        )
        last = slice(SLOTS - PIECE, SLOTS)
        nc.vector.tensor_scalar(out=ahead[:, last], in0=ln_t[:, last], scalar1=ls_sb, scalar2=None, op0=ALU.add)

        diffs = {}

        def subtract(h):
            cols = slice(h * PIECE, (h + 1) * PIECE)
            acc = psum.tile([P, PIECE], F32, name="acc%d" % h)
            nc.tensor.matmul_mx(
                out=acc[:],
                lhsT=q_codes[:].bitcast(FP8X4),
                lhsT_scale=q_scales[:],
                rhs=key_words[:, cols].bitcast(FP8X4),
                rhs_scale=key_scales[:, cols],
                start=True,
                stop=True,
            )
            diffs[h] = keep.tile([P, PIECE], F32, name="diff%d" % h)
            if h < PIECES // 2:
                nc.vector.tensor_tensor(out=diffs[h][:], in0=t_piece(h), in1=acc[:], op=ALU.mult)
            elif h < PIECES - 1:
                nc.vector.scalar_tensor_tensor(
                    out=diffs[h][:], in0=ln_t[:, cols], scalar=ls_sb, in1=acc[:], op0=ALU.add, op1=ALU.subtract
                )
            else:
                nc.vector.tensor_tensor(out=diffs[h][:], in0=ahead[:, cols], in1=acc[:], op=ALU.subtract)

        def weigh(h):
            cols = slice(h * PIECE, (h + 1) * PIECE)
            if h < PIECES // 2:
                nc.vector.tensor_tensor(out=y[:, cols], in0=ahead[:, cols], in1=diffs[h][:], op=ALU.subtract)
            else:
                nc.vector.tensor_tensor(out=y[:, cols], in0=diffs[h][:], in1=t_piece(h), op=ALU.mult)
            queue = nc.scalar if h % 2 == 0 else nc.sync
            queue.dma_start(out=out[0][:, cols], in_=y[:, cols])

        LAG = 2
        for h in range(PIECES + LAG):
            if h < PIECES:
                subtract(h)
            if h >= LAG:
                weigh(h - LAG)
